import numpy as np
import ml_dtypes


def mxq(x, axis, fmt="e4m3"):
    dtype, down = {"e4m3": (ml_dtypes.float8_e4m3fn, 7), "e5m2": (ml_dtypes.float8_e5m2, 14)}[fmt]
    v = np.moveaxis(np.asarray(x, np.float32).astype(ml_dtypes.bfloat16).astype(np.float64), axis, -1)
    blocks = v.reshape(v.shape[:-1] + (-1, 32))
    amax = np.abs(blocks).max(-1, keepdims=True)
    byte = np.maximum(np.where(amax > 0, np.frexp(amax)[1] - 1 + 127, 0) - down, 1)
    scale = np.exp2(byte - 127.0)
    codes = (blocks / scale).astype(np.float32).astype(dtype).astype(np.float64)
    return np.moveaxis((codes * scale).reshape(v.shape), -1, axis)


WIDE = False


def mx_kscale(k):
    if not WIDE:
        return np.ones(k)
    levels = np.array([10, -10, 5, -5, 0])
    if k % 512:
        return np.exp2(np.random.permutation(np.resize(levels, k // 32))).repeat(32)
    a = np.empty((k // 512, 16))
    for p in range(k // 512):
        a[p, :8] = np.random.permutation(np.resize(levels, 8))
        for g in range(8):
            far = levels[np.abs(levels - a[p, g]) >= 10]
            a[p, g + 8] = far[np.random.randint(len(far))]
    return np.exp2(a.ravel()).repeat(32)


def f64(x):
    return np.asarray(x).astype(np.float64)


def striped(idx):
    return np.tile(np.asarray(idx).reshape(-1, 16).T, (8, 1)).astype(np.uint16)


def unstriped(offs):
    return offs[:16].T.reshape(-1).astype(np.int64)


E2M1 = np.array([0.0, 0.5, 1.0, 1.5, 2.0, 3.0, 4.0, 6.0, -0.0, -0.5, -1.0, -1.5, -2.0, -3.0, -4.0, -6.0])


def pack_weight(w, fmt):
    k, n = w.shape
    w = f64(np.asarray(w, np.float32).astype(ml_dtypes.bfloat16)).reshape(k // 32, 32, n)
    amax = np.abs(w).max(1)
    if fmt == "e4m3":
        byte = np.frexp(amax)[1] - 1 + 127 - 7
    else:
        mant, ex = np.frexp(amax / 6.0)
        byte = np.where(mant > 0.5, ex, ex - 1) + 127
    byte = np.clip(np.where(amax > 0, byte, 1), 1, 254)
    scaled = (w * np.exp2(127.0 - byte)[:, None, :]).reshape(k, n).astype(np.float32)
    by_word = np.ascontiguousarray(scaled.reshape(k // 512, 128, 4, n).transpose(0, 1, 3, 2))
    if fmt == "e4m3":
        words = by_word.astype(ml_dtypes.float8_e4m3fn).view(np.uint8)
    else:
        c = by_word.astype(ml_dtypes.float4_e2m1fn).view(np.uint8) & 0xF
        words = (c[..., 0::2] | (c[..., 1::2] << 4)).reshape(k // 512, 128, 2 * n)
    return np.ascontiguousarray(words), np.ascontiguousarray(byte.astype(np.uint8).reshape(k // 512, 16, n))


def unpack_weight(words, scales, fmt):
    g, _, n = scales.shape
    words = np.ascontiguousarray(words).reshape(g, 128, n, -1)
    if fmt == "e4m3":
        vals = words.view(ml_dtypes.float8_e4m3fn).astype(np.float64)
    else:
        nib = np.empty((g, 128, n, 4), np.uint8)
        nib[..., 0::2] = words & 0xF
        nib[..., 1::2] = words >> 4
        vals = E2M1[nib]
    vals = vals * np.repeat(np.exp2(scales.astype(np.float64) - 127.0), 8, axis=1)[..., None]
    return vals.transpose(0, 1, 3, 2).reshape(g * 512, n)


D, E, T, I, Q = 512, 512, 2048, 512, 128


def setup_inputs():
    n = np.random.standard_normal
    idx = np.random.permutation(T)[:I]
    fd = mx_kscale(D)
    fe = mx_kscale(E)
    keysp = pack_weight(n((D, T)) / fd[:, None], "e2m1")
    valsp = pack_weight(n((E, T)) / fe[:, None], "e2m1")
    return {
        "query": (n((D, Q)) * 1.0 / np.sqrt(D) * fd[:, None]).astype(np.float32),
        "keys_words": keysp[0],
        "keys_scales": keysp[1],
        "floor": (np.random.uniform(0.05, 0.3, (Q, 1))).astype(np.float32),
        "reserve": (np.random.uniform(20.0, 100.0, (Q, 1))).astype(np.float32),
        "gout": (n((E, Q)) * 1 / np.sqrt(E) * fe[:, None]).astype(np.float32),
        "vals_words": valsp[0],
        "vals_scales": valsp[1],
        "old": (0.5 * n((Q, T))).astype(np.float32),
        "offs": striped(idx),
    }


def reference(query, keys_words, keys_scales, floor, reserve, gout, vals_words, vals_scales, old, offs):
    idx = unstriped(offs)
    keysu = unpack_weight(keys_words, keys_scales, "e2m1")
    valsu = unpack_weight(vals_words, vals_scales, "e2m1")
    queryq = mxq(f64(query), 0, "e4m3")
    keysidxg = keysu[:, idx]
    a = queryq.T @ keysidxg
    p = np.square(a) + f64(floor)
    z = np.sum(p, axis=1, keepdims=True) + f64(reserve)
    goutq = mxq(f64(gout), 0, "e4m3")
    valsidxg = valsu[:, idx]
    c0 = goutq.T @ valsidxg
    dz = np.sum(c0 * p / np.square(z) * (-1.0), axis=1, keepdims=True)
    dp = c0 / z + dz
    da = dp * a * 2.0
    gs = da * 512.0
    gf = np.zeros((Q, T))
    gf[:, idx] = gs
    y = f64(old) + gf
    return y

@@ -1,0 +1,137 @@
+from contextlib import ExitStack
+
+import concourse.mybir as mybir
+
+D, E, T, I, Q = 512, 512, 2048, 512, 128
+FLOPS = 2 * Q * I * (D + E)
+
+F32 = mybir.dt.float32
+BF16 = mybir.dt.bfloat16
+I32 = mybir.dt.int32
+U32 = mybir.dt.uint32
+U16 = mybir.dt.uint16
+U8 = mybir.dt.uint8
+FP8X4 = mybir.dt.float8_e4m3fn_x4
+FP4X4 = mybir.dt.float4_e2m1fn_x4
+ACT = mybir.ActivationFunctionType
+ALU = mybir.AluOpType
+
+P = 128
+PACK = 4
+HALF = I // 2
+GAIN = 2.0 * 512.0
+STORE_WIDTHS = (512, 512, 512, 512)
+
+
+def load_scale_rows(nc, plane, scales):
+    for r in range(4):
+        nc.sync.dma_start(out=plane[r:P:32, :].bitcast(I32), in_=scales[0, r:16:4, :].bitcast(I32))
+
+
+def quantise(nc, pool, raw, name):
+    grouped = pool.tile([P, Q, PACK], BF16, name=name + "_grouped", align_bytes=64)
+    codes = pool.tile([P, Q], U32, name=name + "_codes", align_bytes=64)
+    scales = pool.tile([P, Q], U8, name=name + "_scales", align_bytes=64)
+    nc.scalar.activation(grouped[:], raw[:].rearrange("p j q -> p q j"), ACT.Copy)
+    nc.vector.quantize_mx(out=codes[:].bitcast(FP8X4), scales=scales[:], in_=grouped[:].rearrange("p q j -> p (q j)"))
+    return codes, scales
+
+
+def tile_attend_bsquareshares_s_kernel(tc, query, keys_words, keys_scales, floor, reserve, gout, vals_words,
+                                        vals_scales, old, offs, out):
+    nc = tc.nc
+    with ExitStack() as ctx:
+        sb = ctx.enter_context(tc.tile_pool(name="sb", bufs=1))
+        ps = ctx.enter_context(tc.psum_pool(name="ps", bufs=1))
+
+        offsets = sb.tile([P, I // 16], U16, name="offsets")
+        kw = sb.tile([P, T], U16, name="kw")
+        ks = sb.tile([P, T], U8, name="ks")
+        vw = sb.tile([P, T], U16, name="vw")
+        vs = sb.tile([P, T], U8, name="vs", tag="vs_then_gain")
+        q_raw = sb.tile([P, PACK, Q], F32, name="q_raw")
+        g_raw = sb.tile([P, PACK, Q], F32, name="g_raw", tag="g_raw_then_sq")
+        floor_sb = sb.tile([P, 1], F32, name="floor_sb")
+        reserve_sb = sb.tile([P, 1], F32, name="reserve_sb")
+        old_sb = sb.tile([P, T], F32, name="old_sb")
+        gf = sb.tile([P, T], F32, name="gf")
+
+        nc.vector.memset(ks[:].bitcast(I32), 0)
+        nc.vector.memset(vs[:].bitcast(I32), 0)
+        nc.vector.memset(gf[:], 0.0)
+
+        nc.sync.dma_start(offsets[:], offs)
+        nc.sync.dma_start(out=kw[:].bitcast(I32), in_=keys_words[0].bitcast(I32))
+        load_scale_rows(nc, ks, keys_scales)
+        nc.sync.dma_start(out=q_raw[:], in_=query.rearrange("(p j) q -> p j q", j=PACK))
+        nc.sync.dma_start(out=vw[:].bitcast(I32), in_=vals_words[0].bitcast(I32))
+        nc.sync.dma_start(out=g_raw[:], in_=gout.rearrange("(p j) q -> p j q", j=PACK))
+        nc.sync.dma_start(out=floor_sb[:], in_=floor)
+        nc.sync.dma_start(out=reserve_sb[:], in_=reserve)
+        load_scale_rows(nc, vs, vals_scales)
+        nc.sync.dma_start(out=old_sb[:], in_=old)
+
+        kw_g = sb.tile([P, I], U16, name="kw_g", align_bytes=64)
+        ks_g = sb.tile([P, I], U8, name="ks_g", align_bytes=64)
+        nc.vector.tensor_copy(kw_g[:], kw[:].indirect(offsets[:]))
+        nc.vector.tensor_copy(ks_g[:], ks[:].indirect(offsets[:]))
+        q_codes, q_scales = quantise(nc, sb, q_raw, "q")
+        a_ps = ps.tile([P, I], F32, name="a_ps")
+        nc.tensor.matmul_mx(out=a_ps[:], lhsT=q_codes[:].bitcast(FP8X4), lhsT_scale=q_scales[:],
+                            rhs=kw_g[:].bitcast(FP4X4), rhs_scale=ks_g[:], start=True, stop=True)
+
+        vw_g = sb.tile([P, I], U16, name="vw_g", align_bytes=64)
+        nc.vector.tensor_copy(vw_g[:], vw[:].indirect(offsets[:]))
+        g_codes, g_scales = quantise(nc, sb, g_raw, "g")
+        c_ps = []
+        for h in range(2):
+            vs_g = sb.tile([P, HALF], U8, name="vs_g%d" % h, align_bytes=64)
+            nc.vector.tensor_copy(vs_g[:], vs[:].indirect(offsets[:, h * HALF // 16:(h + 1) * HALF // 16]))
+            bank = ps.tile([P, HALF], F32, name="c_ps%d" % h)
+            nc.tensor.matmul_mx(out=bank[:], lhsT=g_codes[:].bitcast(FP8X4), lhsT_scale=g_scales[:],
+                                rhs=vw_g[:, h * HALF:(h + 1) * HALF].bitcast(FP4X4), rhs_scale=vs_g[:],
+                                start=True, stop=True)
+            c_ps.append(bank)
+
+        reserve_part = sb.tile([P, 1], F32, name="reserve_part")
+        z_rest = sb.tile([P, 1], F32, name="z_rest")
+        floor_part = sb.tile([P, 1], F32, name="floor_part")
+        nc.scalar.activation(reserve_part[:], reserve_sb[:], ACT.Copy, scale=1.0 / GAIN)
+        nc.scalar.activation(z_rest[:], floor_sb[:], ACT.Identity, scale=I / GAIN, bias=reserve_part[:])
+        nc.scalar.activation(floor_part[:], floor_sb[:], ACT.Copy, scale=-1.0 / GAIN)
+
+        sq = sb.tile([P, I], F32, name="sq", tag="g_raw_then_sq")
+        sq_sum = sb.tile([P, 1], F32, name="sq_sum")
+        z_part = sb.tile([P, 1], F32, name="z_part")
+        p_part = sb.tile([P, I], F32, name="p_part")
+        nc.scalar.activation(sq[:], a_ps[:], ACT.Square, accum_out=sq_sum[:])
+        nc.scalar.activation(z_part[:], sq_sum[:], ACT.Identity, scale=1.0 / GAIN, bias=z_rest[:])
+        nc.scalar.activation(p_part[:], sq[:], ACT.Identity, scale=-1.0 / GAIN, bias=floor_part[:])
+        gain = sb.tile([P, 1], F32, name="gain", tag="vs_then_gain")
+        nc.vector.reciprocal(gain[:], z_part[:])
+        a_gain = sb.tile([P, I], F32, name="a_gain")
+        nc.scalar.activation(a_gain[:], a_ps[:], ACT.Copy, scale=gain[:])
+
+        terms = sb.tile([P, I], F32, name="terms")
+        shift = []
+        for h in range(2):
+            part = sb.tile([P, 1], F32, name="shift%d" % h)
+            cols = slice(h * HALF, (h + 1) * HALF)
+            nc.vector.scalar_tensor_tensor(terms[:, cols], c_ps[h][:], gain[:], p_part[:, cols], ALU.mult, ALU.mult,
+                                           accum_out=part[:])
+            shift.append(part)
+        centred = sb.tile([P, I], F32, name="centred")
+        first = sb.tile([P, HALF], F32, name="first")
+        nc.scalar.activation(first[:], c_ps[0][:], ACT.Identity, bias=shift[0][:])
+        nc.scalar.activation(centred[:, :HALF], first[:], ACT.Identity, bias=shift[1][:])
+        nc.vector.tensor_scalar(centred[:, HALF:], c_ps[1][:], shift[0][:], shift[1][:], ALU.add, ALU.add)
+
+        nc.vector.tensor_tensor(gf[:].indirect(offsets[:]), a_gain[:], centred[:], ALU.mult)
+
+        start = 0
+        for n, width in enumerate(STORE_WIDTHS):
+            cols = slice(start, start + width)
+            res = sb.tile([P, width], F32, name="res%d" % n)
+            nc.vector.tensor_tensor(res[:], gf[:, cols], old_sb[:, cols], ALU.add)
+            nc.sync.dma_start(out=out[:, cols], in_=res[:])
+            start = start + width

@@ -20,7 +20,7 @@ P = 128
 PACK = 4
 HALF = I // 2
 GAIN = 2.0 * 512.0
-STORE_WIDTHS = (512, 512, 512, 512)
+STORE_WIDTHS = (256, 256, 256, 384, 384, 512)
 
 
 def load_scale_rows(nc, plane, scales):
@@ -29,7 +29,7 @@ def load_scale_rows(nc, plane, scales):
 
 
 def quantise(nc, pool, raw, name):
-    grouped = pool.tile([P, Q, PACK], BF16, name=name + "_grouped", align_bytes=64)
+    grouped = pool.tile([P, Q, PACK], BF16, name=name + "_grouped", tag=name + "_grouped", align_bytes=64)
     codes = pool.tile([P, Q], U32, name=name + "_codes", align_bytes=64)
     scales = pool.tile([P, Q], U8, name=name + "_scales", align_bytes=64)
     nc.scalar.activation(grouped[:], raw[:].rearrange("p j q -> p q j"), ACT.Copy)
@@ -48,8 +48,8 @@ def tile_attend_bsquareshares_s_kernel(tc, query, keys_words, keys_scales, floor
         kw = sb.tile([P, T], U16, name="kw")
         ks = sb.tile([P, T], U8, name="ks")
         vw = sb.tile([P, T], U16, name="vw")
-        vs = sb.tile([P, T], U8, name="vs", tag="vs_then_gain")
-        q_raw = sb.tile([P, PACK, Q], F32, name="q_raw")
+        vs = sb.tile([P, T], U8, name="vs")
+        q_raw = sb.tile([P, PACK, Q], F32, name="q_raw", tag="q_raw_then_vw_g", align_bytes=64)
         g_raw = sb.tile([P, PACK, Q], F32, name="g_raw", tag="g_raw_then_sq")
         floor_sb = sb.tile([P, 1], F32, name="floor_sb")
         reserve_sb = sb.tile([P, 1], F32, name="reserve_sb")
@@ -66,8 +66,8 @@ def tile_attend_bsquareshares_s_kernel(tc, query, keys_words, keys_scales, floor
         nc.sync.dma_start(out=q_raw[:], in_=query.rearrange("(p j) q -> p j q", j=PACK))
         nc.sync.dma_start(out=vw[:].bitcast(I32), in_=vals_words[0].bitcast(I32))
         nc.sync.dma_start(out=g_raw[:], in_=gout.rearrange("(p j) q -> p j q", j=PACK))
-        nc.sync.dma_start(out=floor_sb[:], in_=floor)
         nc.sync.dma_start(out=reserve_sb[:], in_=reserve)
+        nc.sync.dma_start(out=floor_sb[:], in_=floor)
         load_scale_rows(nc, vs, vals_scales)
         nc.sync.dma_start(out=old_sb[:], in_=old)
 
@@ -80,51 +80,58 @@ def tile_attend_bsquareshares_s_kernel(tc, query, keys_words, keys_scales, floor
         nc.tensor.matmul_mx(out=a_ps[:], lhsT=q_codes[:].bitcast(FP8X4), lhsT_scale=q_scales[:],
                             rhs=kw_g[:].bitcast(FP4X4), rhs_scale=ks_g[:], start=True, stop=True)
 
-        vw_g = sb.tile([P, I], U16, name="vw_g", align_bytes=64)
+        vw_g = sb.tile([P, I], U16, name="vw_g", tag="q_raw_then_vw_g", align_bytes=64)
         nc.vector.tensor_copy(vw_g[:], vw[:].indirect(offsets[:]))
         g_codes, g_scales = quantise(nc, sb, g_raw, "g")
-        c_ps = []
-        for h in range(2):
-            vs_g = sb.tile([P, HALF], U8, name="vs_g%d" % h, align_bytes=64)
+
+        def values_half(h, tag):
+            vs_g = sb.tile([P, HALF], U8, name="vs_g%d" % h, tag=tag, align_bytes=64)
             nc.vector.tensor_copy(vs_g[:], vs[:].indirect(offsets[:, h * HALF // 16:(h + 1) * HALF // 16]))
             bank = ps.tile([P, HALF], F32, name="c_ps%d" % h)
             nc.tensor.matmul_mx(out=bank[:], lhsT=g_codes[:].bitcast(FP8X4), lhsT_scale=g_scales[:],
                                 rhs=vw_g[:, h * HALF:(h + 1) * HALF].bitcast(FP4X4), rhs_scale=vs_g[:],
                                 start=True, stop=True)
-            c_ps.append(bank)
+            return bank
 
-        reserve_part = sb.tile([P, 1], F32, name="reserve_part")
+        c_ps = [values_half(0, "vs_g0_then_gain"), values_half(1, "vs_g1_then_a_gain")]
+
+        reserve_part = sb.tile([P, 1], F32, name="reserve_part", tag="reserve_part_then_sq_sum")
         z_rest = sb.tile([P, 1], F32, name="z_rest")
         floor_part = sb.tile([P, 1], F32, name="floor_part")
         nc.scalar.activation(reserve_part[:], reserve_sb[:], ACT.Copy, scale=1.0 / GAIN)
-        nc.scalar.activation(z_rest[:], floor_sb[:], ACT.Identity, scale=I / GAIN, bias=reserve_part[:])
         nc.scalar.activation(floor_part[:], floor_sb[:], ACT.Copy, scale=-1.0 / GAIN)
+        nc.scalar.activation(z_rest[:], floor_sb[:], ACT.Identity, scale=I / GAIN, bias=reserve_part[:])
 
         sq = sb.tile([P, I], F32, name="sq", tag="g_raw_then_sq")
-        sq_sum = sb.tile([P, 1], F32, name="sq_sum")
+        sq_sum = sb.tile([P, 1], F32, name="sq_sum", tag="reserve_part_then_sq_sum")
         z_part = sb.tile([P, 1], F32, name="z_part")
         p_part = sb.tile([P, I], F32, name="p_part")
         nc.scalar.activation(sq[:], a_ps[:], ACT.Square, accum_out=sq_sum[:])
         nc.scalar.activation(z_part[:], sq_sum[:], ACT.Identity, scale=1.0 / GAIN, bias=z_rest[:])
-        nc.scalar.activation(p_part[:], sq[:], ACT.Identity, scale=-1.0 / GAIN, bias=floor_part[:])
-        gain = sb.tile([P, 1], F32, name="gain", tag="vs_then_gain")
+        lo, hi = slice(0, HALF), slice(HALF, I)
+        for cols in (lo, hi):
+            nc.scalar.activation(p_part[:, cols], sq[:, cols], ACT.Identity, scale=-1.0 / GAIN, bias=floor_part[:])
+        gain = sb.tile([P, 1], F32, name="gain", tag="vs_g0_then_gain", align_bytes=64)
         nc.vector.reciprocal(gain[:], z_part[:])
-        a_gain = sb.tile([P, I], F32, name="a_gain")
-        nc.scalar.activation(a_gain[:], a_ps[:], ACT.Copy, scale=gain[:])
+        a_sb = sb.tile([P, I], F32, name="a_sb")
+        nc.scalar.copy(a_sb[:], a_ps[:])
 
         terms = sb.tile([P, I], F32, name="terms")
-        shift = []
-        for h in range(2):
-            part = sb.tile([P, 1], F32, name="shift%d" % h)
-            cols = slice(h * HALF, (h + 1) * HALF)
-            nc.vector.scalar_tensor_tensor(terms[:, cols], c_ps[h][:], gain[:], p_part[:, cols], ALU.mult, ALU.mult,
-                                           accum_out=part[:])
-            shift.append(part)
+        sum_lo = sb.tile([P, 1], F32, name="sum_lo")
+        shift_lo = sb.tile([P, 1], F32, name="shift_lo")
+        shift_hi = sb.tile([P, 1], F32, name="shift_hi")
+        nc.vector.scalar_tensor_tensor(terms[:, lo], c_ps[0][:], 1.0, p_part[:, lo], ALU.mult, ALU.mult,
+                                       accum_out=sum_lo[:])
+        nc.vector.scalar_tensor_tensor(terms[:, hi], c_ps[1][:], gain[:], p_part[:, hi], ALU.mult, ALU.mult,
+                                       accum_out=shift_hi[:])
+        c_lo = sb.tile([P, HALF], F32, name="c_lo")
+        nc.scalar.activation(shift_lo[:], sum_lo[:], ACT.Copy, scale=gain[:])
+        nc.scalar.copy(c_lo[:], c_ps[0][:])
+        a_gain = sb.tile([P, I], F32, name="a_gain", tag="vs_g1_then_a_gain", align_bytes=64)
+        nc.vector.tensor_scalar(a_gain[:], a_sb[:], gain[:], None, ALU.mult)
         centred = sb.tile([P, I], F32, name="centred")
-        first = sb.tile([P, HALF], F32, name="first")
-        nc.scalar.activation(first[:], c_ps[0][:], ACT.Identity, bias=shift[0][:])
-        nc.scalar.activation(centred[:, :HALF], first[:], ACT.Identity, bias=shift[1][:])
-        nc.vector.tensor_scalar(centred[:, HALF:], c_ps[1][:], shift[0][:], shift[1][:], ALU.add, ALU.add)
+        nc.vector.tensor_scalar(centred[:, hi], c_ps[1][:], shift_lo[:], shift_hi[:], ALU.add, ALU.add)
+        nc.vector.tensor_scalar(centred[:, lo], c_lo[:], shift_lo[:], shift_hi[:], ALU.add, ALU.add)
 
         nc.vector.tensor_tensor(gf[:].indirect(offsets[:]), a_gain[:], centred[:], ALU.mult)
 

@@ -20,7 +20,7 @@ P = 128
 PACK = 4
 HALF = I // 2
 GAIN = 2.0 * 512.0
-STORE_WIDTHS = (256, 256, 256, 384, 384, 512)
+STORE_WIDTHS = (256,) * 8
 
 
 def load_scale_rows(nc, plane, scales):
@@ -66,9 +66,9 @@ def tile_attend_bsquareshares_s_kernel(tc, query, keys_words, keys_scales, floor
         nc.sync.dma_start(out=q_raw[:], in_=query.rearrange("(p j) q -> p j q", j=PACK))
         nc.sync.dma_start(out=vw[:].bitcast(I32), in_=vals_words[0].bitcast(I32))
         nc.sync.dma_start(out=g_raw[:], in_=gout.rearrange("(p j) q -> p j q", j=PACK))
+        load_scale_rows(nc, vs, vals_scales)
         nc.sync.dma_start(out=reserve_sb[:], in_=reserve)
         nc.sync.dma_start(out=floor_sb[:], in_=floor)
-        load_scale_rows(nc, vs, vals_scales)
         nc.sync.dma_start(out=old_sb[:], in_=old)
 
         kw_g = sb.tile([P, I], U16, name="kw_g", align_bytes=64)
@@ -95,43 +95,37 @@ def tile_attend_bsquareshares_s_kernel(tc, query, keys_words, keys_scales, floor
 
         c_ps = [values_half(0, "vs_g0_then_gain"), values_half(1, "vs_g1_then_a_gain")]
 
-        reserve_part = sb.tile([P, 1], F32, name="reserve_part", tag="reserve_part_then_sq_sum")
-        z_rest = sb.tile([P, 1], F32, name="z_rest")
-        floor_part = sb.tile([P, 1], F32, name="floor_part")
-        nc.scalar.activation(reserve_part[:], reserve_sb[:], ACT.Copy, scale=1.0 / GAIN)
-        nc.scalar.activation(floor_part[:], floor_sb[:], ACT.Copy, scale=-1.0 / GAIN)
-        nc.scalar.activation(z_rest[:], floor_sb[:], ACT.Identity, scale=I / GAIN, bias=reserve_part[:])
-
-        sq = sb.tile([P, I], F32, name="sq", tag="g_raw_then_sq")
-        sq_sum = sb.tile([P, 1], F32, name="sq_sum", tag="reserve_part_then_sq_sum")
-        z_part = sb.tile([P, 1], F32, name="z_part")
-        p_part = sb.tile([P, I], F32, name="p_part")
-        nc.scalar.activation(sq[:], a_ps[:], ACT.Square, accum_out=sq_sum[:])
-        nc.scalar.activation(z_part[:], sq_sum[:], ACT.Identity, scale=1.0 / GAIN, bias=z_rest[:])
         lo, hi = slice(0, HALF), slice(HALF, I)
-        for cols in (lo, hi):
-            nc.scalar.activation(p_part[:, cols], sq[:, cols], ACT.Identity, scale=-1.0 / GAIN, bias=floor_part[:])
-        gain = sb.tile([P, 1], F32, name="gain", tag="vs_g0_then_gain", align_bytes=64)
-        nc.vector.reciprocal(gain[:], z_part[:])
-        a_sb = sb.tile([P, I], F32, name="a_sb")
+        z_rest = sb.tile([P, 1], F32, name="z_rest", tag="z_rest_then_a_sb")
+        sq = sb.tile([P, I], F32, name="sq", tag="g_raw_then_sq")
+        sq_sum = sb.tile([P, 1], F32, name="sq_sum", tag="sq_sum_then_terms")
+        z = sb.tile([P, 1], F32, name="z")
+        p_hi = sb.tile([P, HALF], F32, name="p_hi")
+        nc.scalar.activation(sq[:], a_ps[:], ACT.Square, accum_out=sq_sum[:])
+        nc.scalar.activation(z_rest[:], floor_sb[:], ACT.Identity, scale=float(I), bias=reserve_sb[:])
+        nc.scalar.activation(z[:], sq_sum[:], ACT.Identity, bias=z_rest[:])
+        nc.scalar.activation(p_hi[:], sq[:, hi], ACT.Identity, bias=floor_sb[:])
+        a_sb = sb.tile([P, I], F32, name="a_sb", tag="z_rest_then_a_sb")
         nc.scalar.copy(a_sb[:], a_ps[:])
+        inv_z = sb.tile([P, 1], F32, name="inv_z", tag="vs_g0_then_gain", align_bytes=64)
+        nc.vector.reciprocal(inv_z[:], z[:])
 
-        terms = sb.tile([P, I], F32, name="terms")
+        terms = sb.tile([P, I], F32, name="terms", tag="sq_sum_then_terms")
         sum_lo = sb.tile([P, 1], F32, name="sum_lo")
-        shift_lo = sb.tile([P, 1], F32, name="shift_lo")
-        shift_hi = sb.tile([P, 1], F32, name="shift_hi")
-        nc.vector.scalar_tensor_tensor(terms[:, lo], c_ps[0][:], 1.0, p_part[:, lo], ALU.mult, ALU.mult,
+        mean_lo = sb.tile([P, 1], F32, name="mean_lo")
+        mean_hi = sb.tile([P, 1], F32, name="mean_hi")
+        nc.vector.scalar_tensor_tensor(terms[:, lo], sq[:, lo], floor_sb[:], c_ps[0][:], ALU.add, ALU.mult,
                                        accum_out=sum_lo[:])
-        nc.vector.scalar_tensor_tensor(terms[:, hi], c_ps[1][:], gain[:], p_part[:, hi], ALU.mult, ALU.mult,
-                                       accum_out=shift_hi[:])
+        nc.vector.scalar_tensor_tensor(terms[:, hi], c_ps[1][:], inv_z[:], p_hi[:], ALU.mult, ALU.mult,
+                                       accum_out=mean_hi[:])
         c_lo = sb.tile([P, HALF], F32, name="c_lo")
-        nc.scalar.activation(shift_lo[:], sum_lo[:], ACT.Copy, scale=gain[:])
         nc.scalar.copy(c_lo[:], c_ps[0][:])
+        nc.scalar.activation(mean_lo[:], sum_lo[:], ACT.Copy, scale=inv_z[:])
         a_gain = sb.tile([P, I], F32, name="a_gain", tag="vs_g1_then_a_gain", align_bytes=64)
-        nc.vector.tensor_scalar(a_gain[:], a_sb[:], gain[:], None, ALU.mult)
+        nc.vector.tensor_scalar(a_gain[:], a_sb[:], inv_z[:], GAIN, ALU.mult, ALU.mult)
         centred = sb.tile([P, I], F32, name="centred")
-        nc.vector.tensor_scalar(centred[:, hi], c_ps[1][:], shift_lo[:], shift_hi[:], ALU.add, ALU.add)
-        nc.vector.tensor_scalar(centred[:, lo], c_lo[:], shift_lo[:], shift_hi[:], ALU.add, ALU.add)
+        nc.vector.tensor_scalar(centred[:, hi], c_ps[1][:], mean_lo[:], mean_hi[:], ALU.subtract, ALU.subtract)
+        nc.vector.tensor_scalar(centred[:, lo], c_lo[:], mean_lo[:], mean_hi[:], ALU.subtract, ALU.subtract)
 
         nc.vector.tensor_tensor(gf[:].indirect(offsets[:]), a_gain[:], centred[:], ALU.mult)
 

@@ -18,22 +18,27 @@ ALU = mybir.AluOpType
 
 P = 128
 PACK = 4
+QUADRANT = 32
+BLOCKS = 16
+LIST_ROWS = 16
 HALF = I // 2
 GAIN = 2.0 * 512.0
-STORE_WIDTHS = (256,) * 8
+STORE_WIDTH = 256
 
 
 def load_scale_rows(nc, plane, scales):
-    for r in range(4):
-        nc.sync.dma_start(out=plane[r:P:32, :].bitcast(I32), in_=scales[0, r:16:4, :].bitcast(I32))
+    per_quadrant = BLOCKS * QUADRANT // P
+    for r in range(per_quadrant):
+        nc.sync.dma_start(out=plane[r:P:QUADRANT, :].bitcast(I32),
+                          in_=scales[0, r:BLOCKS:per_quadrant, :].bitcast(I32))
 
 
 def quantise(nc, pool, raw, name):
-    grouped = pool.tile([P, Q, PACK], BF16, name=name + "_grouped", tag=name + "_grouped", align_bytes=64)
+    grouped = pool.tile([P, Q, PACK], BF16, name=name + "_grouped", align_bytes=64)
     codes = pool.tile([P, Q], U32, name=name + "_codes", align_bytes=64)
     scales = pool.tile([P, Q], U8, name=name + "_scales", align_bytes=64)
-    nc.scalar.activation(grouped[:], raw[:].rearrange("p j q -> p q j"), ACT.Copy)
-    nc.vector.quantize_mx(out=codes[:].bitcast(FP8X4), scales=scales[:], in_=grouped[:].rearrange("p q j -> p (q j)"))
+    nc.scalar.activation(grouped[:], raw[:].rearrange("r j q -> r q j"), ACT.Copy)
+    nc.vector.quantize_mx(out=codes[:].bitcast(FP8X4), scales=scales[:], in_=grouped[:].rearrange("r q j -> r (q j)"))
     return codes, scales
 
 
@@ -44,95 +49,98 @@ def tile_attend_bsquareshares_s_kernel(tc, query, keys_words, keys_scales, floor
         sb = ctx.enter_context(tc.tile_pool(name="sb", bufs=1))
         ps = ctx.enter_context(tc.psum_pool(name="ps", bufs=1))
 
-        offsets = sb.tile([P, I // 16], U16, name="offsets")
-        kw = sb.tile([P, T], U16, name="kw")
-        ks = sb.tile([P, T], U8, name="ks")
-        vw = sb.tile([P, T], U16, name="vw")
-        vs = sb.tile([P, T], U8, name="vs")
-        q_raw = sb.tile([P, PACK, Q], F32, name="q_raw", tag="q_raw_then_vw_g", align_bytes=64)
-        g_raw = sb.tile([P, PACK, Q], F32, name="g_raw", tag="g_raw_then_sq")
+        offsets = sb.tile([P, I // LIST_ROWS], U16, name="offsets")
+        key_words = sb.tile([P, T], U16, name="key_words")
+        key_scales = sb.tile([P, T], U8, name="key_scales")
+        val_words = sb.tile([P, T], U16, name="val_words")
+        val_scales = sb.tile([P, T], U8, name="val_scales")
+        q_raw = sb.tile([P, PACK, Q], F32, name="q_raw", tag="q_raw_then_listed_val_words", align_bytes=64)
+        g_raw = sb.tile([P, PACK, Q], F32, name="g_raw", tag="g_raw_then_squares")
         floor_sb = sb.tile([P, 1], F32, name="floor_sb")
         reserve_sb = sb.tile([P, 1], F32, name="reserve_sb")
         old_sb = sb.tile([P, T], F32, name="old_sb")
         gf = sb.tile([P, T], F32, name="gf")
 
-        nc.vector.memset(ks[:].bitcast(I32), 0)
-        nc.vector.memset(vs[:].bitcast(I32), 0)
+        nc.vector.memset(key_scales[:].bitcast(I32), 0)
+        nc.vector.memset(val_scales[:].bitcast(I32), 0)
         nc.vector.memset(gf[:], 0.0)
 
+        nc.sync.dma_start(out=key_words[:].bitcast(I32), in_=keys_words[0].bitcast(I32))
         nc.sync.dma_start(offsets[:], offs)
-        nc.sync.dma_start(out=kw[:].bitcast(I32), in_=keys_words[0].bitcast(I32))
-        load_scale_rows(nc, ks, keys_scales)
-        nc.sync.dma_start(out=q_raw[:], in_=query.rearrange("(p j) q -> p j q", j=PACK))
-        nc.sync.dma_start(out=vw[:].bitcast(I32), in_=vals_words[0].bitcast(I32))
-        nc.sync.dma_start(out=g_raw[:], in_=gout.rearrange("(p j) q -> p j q", j=PACK))
-        load_scale_rows(nc, vs, vals_scales)
+        load_scale_rows(nc, key_scales, keys_scales)
+        nc.sync.dma_start(out=q_raw[:], in_=query.rearrange("(r j) q -> r j q", j=PACK))
+        nc.sync.dma_start(out=val_words[:].bitcast(I32), in_=vals_words[0].bitcast(I32))
+        nc.sync.dma_start(out=g_raw[:], in_=gout.rearrange("(r j) q -> r j q", j=PACK))
+        load_scale_rows(nc, val_scales, vals_scales)
         nc.sync.dma_start(out=reserve_sb[:], in_=reserve)
         nc.sync.dma_start(out=floor_sb[:], in_=floor)
         nc.sync.dma_start(out=old_sb[:], in_=old)
 
-        kw_g = sb.tile([P, I], U16, name="kw_g", align_bytes=64)
-        ks_g = sb.tile([P, I], U8, name="ks_g", align_bytes=64)
-        nc.vector.tensor_copy(kw_g[:], kw[:].indirect(offsets[:]))
-        nc.vector.tensor_copy(ks_g[:], ks[:].indirect(offsets[:]))
+        listed_key_words = sb.tile([P, I], U16, name="listed_key_words", align_bytes=64)
+        listed_key_scales = sb.tile([P, I], U8, name="listed_key_scales", align_bytes=64)
+        nc.vector.tensor_copy(listed_key_words[:], key_words[:].indirect(offsets[:]))
+        nc.vector.tensor_copy(listed_key_scales[:], key_scales[:].indirect(offsets[:]))
         q_codes, q_scales = quantise(nc, sb, q_raw, "q")
         a_ps = ps.tile([P, I], F32, name="a_ps")
         nc.tensor.matmul_mx(out=a_ps[:], lhsT=q_codes[:].bitcast(FP8X4), lhsT_scale=q_scales[:],
-                            rhs=kw_g[:].bitcast(FP4X4), rhs_scale=ks_g[:], start=True, stop=True)
+                            rhs=listed_key_words[:].bitcast(FP4X4), rhs_scale=listed_key_scales[:],
+                            start=True, stop=True)
 
-        vw_g = sb.tile([P, I], U16, name="vw_g", tag="q_raw_then_vw_g", align_bytes=64)
-        nc.vector.tensor_copy(vw_g[:], vw[:].indirect(offsets[:]))
+        listed_val_words = sb.tile([P, I], U16, name="listed_val_words", tag="q_raw_then_listed_val_words",
+                                   align_bytes=64)
+        nc.vector.tensor_copy(listed_val_words[:], val_words[:].indirect(offsets[:]))
         g_codes, g_scales = quantise(nc, sb, g_raw, "g")
 
-        def values_half(h, tag):
-            vs_g = sb.tile([P, HALF], U8, name="vs_g%d" % h, tag=tag, align_bytes=64)
-            nc.vector.tensor_copy(vs_g[:], vs[:].indirect(offsets[:, h * HALF // 16:(h + 1) * HALF // 16]))
-            bank = ps.tile([P, HALF], F32, name="c_ps%d" % h)
+        def c0_half(slots, name, tag):
+            listed_scales = sb.tile([P, HALF], U8, name="listed_val_scales_" + name, tag=tag, align_bytes=64)
+            entries = offsets[:, slots.start // LIST_ROWS:slots.stop // LIST_ROWS]
+            nc.vector.tensor_copy(listed_scales[:], val_scales[:].indirect(entries))
+            bank = ps.tile([P, HALF], F32, name="c0_" + name)
             nc.tensor.matmul_mx(out=bank[:], lhsT=g_codes[:].bitcast(FP8X4), lhsT_scale=g_scales[:],
-                                rhs=vw_g[:, h * HALF:(h + 1) * HALF].bitcast(FP4X4), rhs_scale=vs_g[:],
+                                rhs=listed_val_words[:, slots].bitcast(FP4X4), rhs_scale=listed_scales[:],
                                 start=True, stop=True)
             return bank
 
-        c_ps = [values_half(0, "vs_g0_then_gain"), values_half(1, "vs_g1_then_a_gain")]
-
         lo, hi = slice(0, HALF), slice(HALF, I)
+        c0_lo = c0_half(lo, "lo", "listed_val_scales_lo_then_inv_z")
+        c0_hi = c0_half(hi, "hi", "listed_val_scales_hi_then_a_gain")
+
         z_rest = sb.tile([P, 1], F32, name="z_rest", tag="z_rest_then_a_sb")
-        sq = sb.tile([P, I], F32, name="sq", tag="g_raw_then_sq")
-        sq_sum = sb.tile([P, 1], F32, name="sq_sum", tag="sq_sum_then_terms")
+        squares = sb.tile([P, I], F32, name="squares", tag="g_raw_then_squares")
+        squares_sum = sb.tile([P, 1], F32, name="squares_sum", tag="squares_sum_then_terms")
         z = sb.tile([P, 1], F32, name="z")
         p_hi = sb.tile([P, HALF], F32, name="p_hi")
-        nc.scalar.activation(sq[:], a_ps[:], ACT.Square, accum_out=sq_sum[:])
+        nc.scalar.activation(squares[:], a_ps[:], ACT.Square, accum_out=squares_sum[:])
         nc.scalar.activation(z_rest[:], floor_sb[:], ACT.Identity, scale=float(I), bias=reserve_sb[:])
-        nc.scalar.activation(z[:], sq_sum[:], ACT.Identity, bias=z_rest[:])
-        nc.scalar.activation(p_hi[:], sq[:, hi], ACT.Identity, bias=floor_sb[:])
+        nc.scalar.activation(z[:], squares_sum[:], ACT.Identity, bias=z_rest[:])
+        nc.scalar.activation(p_hi[:], squares[:, hi], ACT.Identity, bias=floor_sb[:])
         a_sb = sb.tile([P, I], F32, name="a_sb", tag="z_rest_then_a_sb")
         nc.scalar.copy(a_sb[:], a_ps[:])
-        inv_z = sb.tile([P, 1], F32, name="inv_z", tag="vs_g0_then_gain", align_bytes=64)
+        inv_z = sb.tile([P, 1], F32, name="inv_z", tag="listed_val_scales_lo_then_inv_z", align_bytes=64)
         nc.vector.reciprocal(inv_z[:], z[:])
 
-        terms = sb.tile([P, I], F32, name="terms", tag="sq_sum_then_terms")
+        terms = sb.tile([P, I], F32, name="terms", tag="squares_sum_then_terms")
         sum_lo = sb.tile([P, 1], F32, name="sum_lo")
         mean_lo = sb.tile([P, 1], F32, name="mean_lo")
         mean_hi = sb.tile([P, 1], F32, name="mean_hi")
-        nc.vector.scalar_tensor_tensor(terms[:, lo], sq[:, lo], floor_sb[:], c_ps[0][:], ALU.add, ALU.mult,
+        nc.vector.scalar_tensor_tensor(terms[:, lo], squares[:, lo], floor_sb[:], c0_lo[:], ALU.add, ALU.mult,
                                        accum_out=sum_lo[:])
-        nc.vector.scalar_tensor_tensor(terms[:, hi], c_ps[1][:], inv_z[:], p_hi[:], ALU.mult, ALU.mult,
+        nc.vector.scalar_tensor_tensor(terms[:, hi], c0_hi[:], inv_z[:], p_hi[:], ALU.mult, ALU.mult,
                                        accum_out=mean_hi[:])
-        c_lo = sb.tile([P, HALF], F32, name="c_lo")
-        nc.scalar.copy(c_lo[:], c_ps[0][:])
+        c0_lo_sb = sb.tile([P, HALF], F32, name="c0_lo_sb")
+        nc.scalar.copy(c0_lo_sb[:], c0_lo[:])
         nc.scalar.activation(mean_lo[:], sum_lo[:], ACT.Copy, scale=inv_z[:])
-        a_gain = sb.tile([P, I], F32, name="a_gain", tag="vs_g1_then_a_gain", align_bytes=64)
+
+        a_gain = sb.tile([P, I], F32, name="a_gain", tag="listed_val_scales_hi_then_a_gain", align_bytes=64)
         nc.vector.tensor_scalar(a_gain[:], a_sb[:], inv_z[:], GAIN, ALU.mult, ALU.mult)
         centred = sb.tile([P, I], F32, name="centred")
-        nc.vector.tensor_scalar(centred[:, hi], c_ps[1][:], mean_lo[:], mean_hi[:], ALU.subtract, ALU.subtract)
-        nc.vector.tensor_scalar(centred[:, lo], c_lo[:], mean_lo[:], mean_hi[:], ALU.subtract, ALU.subtract)
+        nc.vector.tensor_scalar(centred[:, hi], c0_hi[:], mean_lo[:], mean_hi[:], ALU.subtract, ALU.subtract)
+        nc.vector.tensor_scalar(centred[:, lo], c0_lo_sb[:], mean_lo[:], mean_hi[:], ALU.subtract, ALU.subtract)
 
         nc.vector.tensor_tensor(gf[:].indirect(offsets[:]), a_gain[:], centred[:], ALU.mult)
 
-        start = 0
-        for n, width in enumerate(STORE_WIDTHS):
-            cols = slice(start, start + width)
-            res = sb.tile([P, width], F32, name="res%d" % n)
-            nc.vector.tensor_tensor(res[:], gf[:, cols], old_sb[:, cols], ALU.add)
-            nc.sync.dma_start(out=out[:, cols], in_=res[:])
-            start = start + width
+        for start in range(0, T, STORE_WIDTH):
+            cols = slice(start, start + STORE_WIDTH)
+            total = sb.tile([P, STORE_WIDTH], F32, name="total_%d" % start)
+            nc.vector.tensor_tensor(total[:], gf[:, cols], old_sb[:, cols], ALU.add)
+            nc.sync.dma_start(out=out[:, cols], in_=total[:])

from contextlib import ExitStack

import concourse.mybir as mybir

D, E, T, I, Q = 512, 512, 2048, 512, 128
FLOPS = 2 * Q * I * (D + E)

F32 = mybir.dt.float32
BF16 = mybir.dt.bfloat16
I32 = mybir.dt.int32
U32 = mybir.dt.uint32
U16 = mybir.dt.uint16
U8 = mybir.dt.uint8
FP8X4 = mybir.dt.float8_e4m3fn_x4
FP4X4 = mybir.dt.float4_e2m1fn_x4
ACT = mybir.ActivationFunctionType
ALU = mybir.AluOpType

P = 128
PACK = 4
QUADRANT = 32
BLOCKS = 16
LIST_ROWS = 16
HALF = I // 2
GAIN = 2.0 * 512.0
STORE_WIDTH = 256


def load_scale_rows(nc, plane, scales):
    per_quadrant = BLOCKS * QUADRANT // P
    for r in range(per_quadrant):
        nc.sync.dma_start(out=plane[r:P:QUADRANT, :].bitcast(I32),
                          in_=scales[0, r:BLOCKS:per_quadrant, :].bitcast(I32))


def quantise(nc, pool, raw, name):
    grouped = pool.tile([P, Q, PACK], BF16, name=name + "_grouped", align_bytes=64)
    codes = pool.tile([P, Q], U32, name=name + "_codes", align_bytes=64)
    scales = pool.tile([P, Q], U8, name=name + "_scales", align_bytes=64)
    nc.scalar.activation(grouped[:], raw[:].rearrange("r j q -> r q j"), ACT.Copy)
    nc.vector.quantize_mx(out=codes[:].bitcast(FP8X4), scales=scales[:], in_=grouped[:].rearrange("r q j -> r (q j)"))
    return codes, scales


def tile_attend_bsquareshares_s_kernel(tc, query, keys_words, keys_scales, floor, reserve, gout, vals_words,
                                        vals_scales, old, offs, out):
    nc = tc.nc
    with ExitStack() as ctx:
        sb = ctx.enter_context(tc.tile_pool(name="sb", bufs=1))
        ps = ctx.enter_context(tc.psum_pool(name="ps", bufs=1))

        offsets = sb.tile([P, I // LIST_ROWS], U16, name="offsets")
        key_words = sb.tile([P, T], U16, name="key_words")
        key_scales = sb.tile([P, T], U8, name="key_scales")
        val_words = sb.tile([P, T], U16, name="val_words")
        val_scales = sb.tile([P, T], U8, name="val_scales")
        q_raw = sb.tile([P, PACK, Q], F32, name="q_raw", tag="q_raw_then_listed_val_words", align_bytes=64)
        g_raw = sb.tile([P, PACK, Q], F32, name="g_raw", tag="g_raw_then_squares")
        floor_sb = sb.tile([P, 1], F32, name="floor_sb")
        reserve_sb = sb.tile([P, 1], F32, name="reserve_sb")
        old_sb = sb.tile([P, T], F32, name="old_sb")
        gf = sb.tile([P, T], F32, name="gf")

        nc.vector.memset(key_scales[:].bitcast(I32), 0)
        nc.vector.memset(val_scales[:].bitcast(I32), 0)
        nc.vector.memset(gf[:], 0.0)

        nc.sync.dma_start(out=key_words[:].bitcast(I32), in_=keys_words[0].bitcast(I32))
        nc.sync.dma_start(offsets[:], offs)
        load_scale_rows(nc, key_scales, keys_scales)
        nc.sync.dma_start(out=q_raw[:], in_=query.rearrange("(r j) q -> r j q", j=PACK))
        nc.sync.dma_start(out=val_words[:].bitcast(I32), in_=vals_words[0].bitcast(I32))
        nc.sync.dma_start(out=g_raw[:], in_=gout.rearrange("(r j) q -> r j q", j=PACK))
        load_scale_rows(nc, val_scales, vals_scales)
        nc.sync.dma_start(out=reserve_sb[:], in_=reserve)
        nc.sync.dma_start(out=floor_sb[:], in_=floor)
        nc.sync.dma_start(out=old_sb[:], in_=old)

        listed_key_words = sb.tile([P, I], U16, name="listed_key_words", align_bytes=64)
        listed_key_scales = sb.tile([P, I], U8, name="listed_key_scales", align_bytes=64)
        nc.vector.tensor_copy(listed_key_words[:], key_words[:].indirect(offsets[:]))
        nc.vector.tensor_copy(listed_key_scales[:], key_scales[:].indirect(offsets[:]))
        q_codes, q_scales = quantise(nc, sb, q_raw, "q")
        a_ps = ps.tile([P, I], F32, name="a_ps")
        nc.tensor.matmul_mx(out=a_ps[:], lhsT=q_codes[:].bitcast(FP8X4), lhsT_scale=q_scales[:],
                            rhs=listed_key_words[:].bitcast(FP4X4), rhs_scale=listed_key_scales[:],
                            start=True, stop=True)

        listed_val_words = sb.tile([P, I], U16, name="listed_val_words", tag="q_raw_then_listed_val_words",
                                   align_bytes=64)
        nc.vector.tensor_copy(listed_val_words[:], val_words[:].indirect(offsets[:]))
        g_codes, g_scales = quantise(nc, sb, g_raw, "g")

        def c0_half(slots, name, tag):
            listed_scales = sb.tile([P, HALF], U8, name="listed_val_scales_" + name, tag=tag, align_bytes=64)
            entries = offsets[:, slots.start // LIST_ROWS:slots.stop // LIST_ROWS]
            nc.vector.tensor_copy(listed_scales[:], val_scales[:].indirect(entries))
            bank = ps.tile([P, HALF], F32, name="c0_" + name)
            nc.tensor.matmul_mx(out=bank[:], lhsT=g_codes[:].bitcast(FP8X4), lhsT_scale=g_scales[:],
                                rhs=listed_val_words[:, slots].bitcast(FP4X4), rhs_scale=listed_scales[:],
                                start=True, stop=True)
            return bank

        lo, hi = slice(0, HALF), slice(HALF, I)
        c0_lo = c0_half(lo, "lo", "listed_val_scales_lo_then_inv_z")
        c0_hi = c0_half(hi, "hi", "listed_val_scales_hi_then_a_gain")

        z_rest = sb.tile([P, 1], F32, name="z_rest", tag="z_rest_then_a_sb")
        squares = sb.tile([P, I], F32, name="squares", tag="g_raw_then_squares")
        squares_sum = sb.tile([P, 1], F32, name="squares_sum", tag="squares_sum_then_terms")
        z = sb.tile([P, 1], F32, name="z")
        p_hi = sb.tile([P, HALF], F32, name="p_hi")
        nc.scalar.activation(squares[:], a_ps[:], ACT.Square, accum_out=squares_sum[:])
        nc.scalar.activation(z_rest[:], floor_sb[:], ACT.Identity, scale=float(I), bias=reserve_sb[:])
        nc.scalar.activation(z[:], squares_sum[:], ACT.Identity, bias=z_rest[:])
        nc.scalar.activation(p_hi[:], squares[:, hi], ACT.Identity, bias=floor_sb[:])
        a_sb = sb.tile([P, I], F32, name="a_sb", tag="z_rest_then_a_sb")
        nc.scalar.copy(a_sb[:], a_ps[:])
        inv_z = sb.tile([P, 1], F32, name="inv_z", tag="listed_val_scales_lo_then_inv_z", align_bytes=64)
        nc.vector.reciprocal(inv_z[:], z[:])

        terms = sb.tile([P, I], F32, name="terms", tag="squares_sum_then_terms")
        sum_lo = sb.tile([P, 1], F32, name="sum_lo")
        mean_lo = sb.tile([P, 1], F32, name="mean_lo")
        mean_hi = sb.tile([P, 1], F32, name="mean_hi")
        nc.vector.scalar_tensor_tensor(terms[:, lo], squares[:, lo], floor_sb[:], c0_lo[:], ALU.add, ALU.mult,
                                       accum_out=sum_lo[:])
        nc.vector.scalar_tensor_tensor(terms[:, hi], c0_hi[:], inv_z[:], p_hi[:], ALU.mult, ALU.mult,
                                       accum_out=mean_hi[:])
        c0_lo_sb = sb.tile([P, HALF], F32, name="c0_lo_sb")
        nc.scalar.copy(c0_lo_sb[:], c0_lo[:])
        nc.scalar.activation(mean_lo[:], sum_lo[:], ACT.Copy, scale=inv_z[:])

        a_gain = sb.tile([P, I], F32, name="a_gain", tag="listed_val_scales_hi_then_a_gain", align_bytes=64)
        nc.vector.tensor_scalar(a_gain[:], a_sb[:], inv_z[:], GAIN, ALU.mult, ALU.mult)
        centred = sb.tile([P, I], F32, name="centred")
        nc.vector.tensor_scalar(centred[:, hi], c0_hi[:], mean_lo[:], mean_hi[:], ALU.subtract, ALU.subtract)
        nc.vector.tensor_scalar(centred[:, lo], c0_lo_sb[:], mean_lo[:], mean_hi[:], ALU.subtract, ALU.subtract)

        nc.vector.tensor_tensor(gf[:].indirect(offsets[:]), a_gain[:], centred[:], ALU.mult)

        for start in range(0, T, STORE_WIDTH):
            cols = slice(start, start + STORE_WIDTH)
            total = sb.tile([P, STORE_WIDTH], F32, name="total_%d" % start)
            nc.vector.tensor_tensor(total[:], gf[:, cols], old_sb[:, cols], ALU.add)
            nc.sync.dma_start(out=out[:, cols], in_=total[:])
